import numpy as np, ml_dtypes
CORES = [2,3,42,43,82,83,122,123]
N = 8
F, TK = 128, 128
def setup_inputs(rng):
    return {"x": rng.standard_normal((N, 128, N * TK), dtype=np.float32).astype(ml_dtypes.bfloat16), "w": rng.standard_normal((N, 128, F), dtype=np.float32).astype(ml_dtypes.bfloat16)}
def setup_inputs_big(rng):
    d = setup_inputs(rng)
    for k in ("x", "w"): d[k] = (d[k].astype(np.float32) * 1024.0).astype(d[k].dtype)
    return d
def setup_inputs_small(rng):
    d = setup_inputs(rng)
    for k in ("x", "w"): d[k] = (d[k].astype(np.float32) * (1 / 1024.0)).astype(d[k].dtype)
    return d
def reference(x, w):
    X, W = x.astype(np.float64), w.astype(np.float64)
    y = np.zeros((N, F, N * TK))
    for r in range(N):
        for j in range(N):
            y[r][:, TK * j:TK * j + TK] = W[r].T @ X[j][:, TK * r:TK * r + TK]
    return {"y": y.astype(ml_dtypes.bfloat16 if x.dtype != np.float64 else np.float64)}

@@ -1,0 +1,121 @@
+from concourse.bass import DstId, RemoteDMATransfer
+
+N = 8
+B = 128
+HALF = N // 2
+
+SCRATCH = {
+    "xs": ("sbuf", [128, N * B], "bfloat16"),
+    "ws": ("sbuf", [128, B], "bfloat16"),
+    "land": ("sbuf", [128, N * B], "bfloat16"),
+    "ys": ("sbuf", [128, N * B], "bfloat16"),
+    "p_own": ("psum", [128, 512], "float32"),
+    "p_nb": ("psum", [128, 512], "float32"),
+    "p_far": ("psum", [128, 512], "float32"),
+    "p_near": ("psum", [128, 512], "float32"),
+}
+SEMAPHORES = ["ld_far", "ld_own", "ld_w", "sent", "arr_far", "arr_near", "arr_nb",
+              "mm_own", "mm_nb", "mm_far", "mm_near", "cp_own", "cp_nb", "cp_far", "cp_near",
+              "st_loc", "st_far", "st_near"]
+
+
+def _bits(mask):
+    return [b for b in range(16) if (mask >> b) & 1]
+
+
+def _mask(engines):
+    m = 0
+    for b in engines:
+        m |= 1 << b
+    return m
+
+
+def _cols(ranks):
+    lo, hi = min(ranks), max(ranks)
+    assert hi - lo + 1 == len(ranks)
+    return slice(lo * B, (hi + 1) * B)
+
+
+def _plan(rank, cores, topo):
+    me = cores[rank]
+    h = rank // HALF
+    own_half = list(range(h * HALF, (h + 1) * HALF))
+    far = [r for r in range(N) if r not in own_half]
+    near = [r for r in own_half if topo.chip(cores[r]) != topo.chip(me)]
+    nb = [r for r in own_half if r != rank and topo.chip(cores[r]) == topo.chip(me)]
+    assert all(topo.chip(cores[r]) != topo.chip(me) for r in far)
+    assert all(topo.may_write(me, cores[r]) for r in range(N) if r != rank)
+    assert len(nb) == 1 and len(near) == 2
+    return far, near, nb
+
+
+def rank_program(g, core, T, topo):
+    rank = T.rank_of(core)
+    if rank is None:
+        return
+    cores = list(T.cores)
+    S = T.sem
+    far, near, nb = _plan(rank, cores, topo)
+    own_half = sorted(near + nb + [rank])
+
+    off = _bits(topo.mask(core, cores[far[0]]))
+    for r in far + near:
+        assert _bits(topo.mask(core, cores[r])) == off
+    on = [b for b in _bits(topo.mask(core, cores[nb[0]])) if b not in off]
+    e_far = len(off) // len(far)
+    e_near = len(off) // len(near)
+    e_nb = min(4, len(on))
+
+    def write(dst_rank, engines, sem):
+        rid, pid, _ = topo.addr(cores[dst_rank])
+        return RemoteDMATransfer(dst_ids=[DstId(rid=rid, pnc=pid)], dma_engine_mask=_mask(engines), remote_sem=sem,
+                                 src=T.xs[:, dst_rank * B:(dst_rank + 1) * B],
+                                 dst=T.land[:, rank * B:(rank + 1) * B])
+
+    c_far, c_ownh, c_near = _cols(far), _cols(own_half), _cols(near)
+    c_loc = _cols(nb + [rank])
+    c_me, c_nb = _cols([rank]), _cols(nb)
+
+    g.sync.dma_start(T.xs[:, c_far], T.x[:, c_far]).then_inc(S.ld_far, 16)
+    g.sync.dma_start(T.xs[:, c_ownh], T.x[:, c_ownh]).then_inc(S.ld_own, 16)
+    g.scalar.dma_start(T.ws[:], T.w[:]).then_inc(S.ld_w, 16)
+
+    g.wait_ge(S.ld_far, 16)
+    g.remote_dma_fused([write(r, off[i * e_far:(i + 1) * e_far], S.arr_far) for i, r in enumerate(far)],
+                       local_sem=S.sent)
+    g.wait_ge(S.ld_own, 16)
+    g.remote_dma_fused([write(r, off[i * e_near:(i + 1) * e_near], S.arr_near) for i, r in enumerate(near)]
+                       + [write(nb[0], on[:e_nb], S.arr_nb)], local_sem=S.sent)
+
+    te, ve = g.tensor, g.vector
+    te.wait_ge(S.ld_w, 16)
+    te.wait_ge(S.ld_own, 16)
+    te.matmul(T.p_own[:, 0:B], T.ws[:], T.xs[:, c_me], True, True).then_inc(S.mm_own, 1)
+    te.wait_ge(S.arr_nb, e_nb)
+    te.matmul(T.p_nb[:, 0:B], T.ws[:], T.land[:, c_nb], True, True).then_inc(S.mm_nb, 1)
+    te.wait_ge(S.arr_far, e_far * len(far))
+    te.matmul(T.p_far[:, 0:len(far) * B], T.ws[:], T.land[:, c_far], True, True).then_inc(S.mm_far, 1)
+    te.wait_ge(S.arr_near, e_near * len(near))
+    te.matmul(T.p_near[:, 0:len(near) * B], T.ws[:], T.land[:, c_near], True, True).then_inc(S.mm_near, 1)
+
+    ve.wait_ge(S.mm_own, 1)
+    ve.tensor_copy(T.ys[:, c_me], T.p_own[:, 0:B]).then_inc(S.cp_own, 1)
+    ve.wait_ge(S.mm_nb, 1)
+    ve.tensor_copy(T.ys[:, c_nb], T.p_nb[:, 0:B]).then_inc(S.cp_nb, 1)
+    ve.wait_ge(S.mm_far, 1)
+    ve.tensor_copy(T.ys[:, c_far], T.p_far[:, 0:len(far) * B]).then_inc(S.cp_far, 1)
+    ve.wait_ge(S.mm_near, 1)
+    ve.tensor_copy(T.ys[:, c_near], T.p_near[:, 0:len(near) * B]).then_inc(S.cp_near, 1)
+
+    g.scalar.wait_ge(S.cp_own, 1)
+    g.scalar.wait_ge(S.cp_nb, 1)
+    g.scalar.dma_start(T.y[:, c_loc], T.ys[:, c_loc]).then_inc(S.st_loc, 16)
+    g.sync.wait_ge(S.cp_far, 1)
+    g.sync.dma_start(T.y[:, c_far], T.ys[:, c_far]).then_inc(S.st_far, 16)
+    g.sync.wait_ge(S.cp_near, 1)
+    g.sync.dma_start(T.y[:, c_near], T.ys[:, c_near]).then_inc(S.st_near, 16)
+
+    g.wait_ge(S.sent, e_far * len(far) + e_near * len(near) + e_nb)
+    g.scalar.wait_ge(S.st_loc, 16)
+    g.sync.wait_ge(S.st_far, 16)
+    g.sync.wait_ge(S.st_near, 16)

@@ -2,21 +2,19 @@ from concourse.bass import DstId, RemoteDMATransfer
 
 N = 8
 B = 128
-HALF = N // 2
+GROUPS = ["own", "ga", "nb", "gb", "c1", "c2"]
 
 SCRATCH = {
     "xs": ("sbuf", [128, N * B], "bfloat16"),
     "ws": ("sbuf", [128, B], "bfloat16"),
     "land": ("sbuf", [128, N * B], "bfloat16"),
     "ys": ("sbuf", [128, N * B], "bfloat16"),
-    "p_own": ("psum", [128, 512], "float32"),
-    "p_nb": ("psum", [128, 512], "float32"),
-    "p_far": ("psum", [128, 512], "float32"),
-    "p_near": ("psum", [128, 512], "float32"),
 }
-SEMAPHORES = ["ld_far", "ld_own", "ld_w", "sent", "arr_far", "arr_near", "arr_nb",
-              "mm_own", "mm_nb", "mm_far", "mm_near", "cp_own", "cp_nb", "cp_far", "cp_near",
-              "st_loc", "st_far", "st_near"]
+for _n in GROUPS:
+    SCRATCH["p_" + _n] = ("psum", [128, 512], "float32")
+SEMAPHORES = (["ld_a", "ld_own", "ld_c", "ld_w", "sent", "st_loc"]
+              + ["arr_" + n for n in GROUPS[1:]] + ["mm_" + n for n in GROUPS] + ["cp_" + n for n in GROUPS]
+              + ["st_" + n for n in GROUPS if n not in ("own", "nb")])
 
 
 def _bits(mask):
@@ -37,16 +35,20 @@ def _cols(ranks):
 
 
 def _plan(rank, cores, topo):
-    me = cores[rank]
-    h = rank // HALF
-    own_half = list(range(h * HALF, (h + 1) * HALF))
-    far = [r for r in range(N) if r not in own_half]
-    near = [r for r in own_half if topo.chip(cores[r]) != topo.chip(me)]
-    nb = [r for r in own_half if r != rank and topo.chip(cores[r]) == topo.chip(me)]
-    assert all(topo.chip(cores[r]) != topo.chip(me) for r in far)
-    assert all(topo.may_write(me, cores[r]) for r in range(N) if r != rank)
-    assert len(nb) == 1 and len(near) == 2
-    return far, near, nb
+    chips = []
+    for c in cores:
+        if topo.chip(c) not in chips:
+            chips.append(topo.chip(c))
+    members = [[r for r in range(N) if topo.chip(cores[r]) == ch] for ch in chips]
+    assert len(chips) == 4 and all(len(m) == 2 for m in members)
+
+    def hops(d):
+        return max(1 if topo.same_plane(chips[i], chips[i ^ d]) or topo.mates(chips[i], chips[i ^ d]) else 2
+                   for i in range(4))
+
+    rounds = sorted([1, 2, 3], key=lambda d: (-hops(d), -d))
+    i = chips.index(topo.chip(cores[rank]))
+    return members[i], [members[i ^ d] for d in rounds], members[i].index(rank)
 
 
 def rank_program(g, core, T, topo):
@@ -55,67 +57,61 @@ def rank_program(g, core, T, topo):
         return
     cores = list(T.cores)
     S = T.sem
-    far, near, nb = _plan(rank, cores, topo)
-    own_half = sorted(near + nb + [rank])
+    home, (pa, pb, pc), pos = _plan(rank, cores, topo)
+    nb = home[1 - pos]
+    assert all(topo.may_write(core, cores[r]) for r in range(N) if r != rank)
 
-    off = _bits(topo.mask(core, cores[far[0]]))
-    for r in far + near:
-        assert _bits(topo.mask(core, cores[r])) == off
-    on = [b for b in _bits(topo.mask(core, cores[nb[0]])) if b not in off]
-    e_far = len(off) // len(far)
-    e_near = len(off) // len(near)
-    e_nb = min(4, len(on))
+    off = _bits(topo.mask(core, cores[pa[0]]))
+    assert all(_bits(topo.mask(core, cores[r])) == off for r in pa + pb + pc)
+    on = [b for b in _bits(topo.mask(core, cores[nb])) if b not in off][:4]
+    h = len(off) // 2
 
     def write(dst_rank, engines, sem):
         rid, pid, _ = topo.addr(cores[dst_rank])
         return RemoteDMATransfer(dst_ids=[DstId(rid=rid, pnc=pid)], dma_engine_mask=_mask(engines), remote_sem=sem,
-                                 src=T.xs[:, dst_rank * B:(dst_rank + 1) * B],
-                                 dst=T.land[:, rank * B:(rank + 1) * B])
+                                 src=T.xs[:, _cols([dst_rank])], dst=T.land[:, _cols([rank])])
 
-    c_far, c_ownh, c_near = _cols(far), _cols(own_half), _cols(near)
-    c_loc = _cols(nb + [rank])
-    c_me, c_nb = _cols([rank]), _cols(nb)
+    for ranks, sem in ((pa, S.ld_a), (home + pb, S.ld_own), (pc, S.ld_c)):
+        g.sync.dma_start(T.xs[:, _cols(ranks)], T.x[:, _cols(ranks)]).then_inc(sem, 16)
+    g.sync.dma_start(T.ws[:], T.w[:]).then_inc(S.ld_w, 16)
 
-    g.sync.dma_start(T.xs[:, c_far], T.x[:, c_far]).then_inc(S.ld_far, 16)
-    g.sync.dma_start(T.xs[:, c_ownh], T.x[:, c_ownh]).then_inc(S.ld_own, 16)
-    g.scalar.dma_start(T.ws[:], T.w[:]).then_inc(S.ld_w, 16)
-
-    g.wait_ge(S.ld_far, 16)
-    g.remote_dma_fused([write(r, off[i * e_far:(i + 1) * e_far], S.arr_far) for i, r in enumerate(far)],
-                       local_sem=S.sent)
+    g.wait_ge(S.ld_a, 16)
+    g.remote_dma_fused([write(pa[0], off[:h], S.arr_ga), write(pa[1], off[h:], S.arr_ga)], local_sem=S.sent)
     g.wait_ge(S.ld_own, 16)
-    g.remote_dma_fused([write(r, off[i * e_near:(i + 1) * e_near], S.arr_near) for i, r in enumerate(near)]
-                       + [write(nb[0], on[:e_nb], S.arr_nb)], local_sem=S.sent)
+    g.remote_dma_fused([write(pb[0], off[:h], S.arr_gb), write(pb[1], off[h:], S.arr_gb), write(nb, on, S.arr_nb)],
+                       local_sem=S.sent)
+    g.wait_ge(S.ld_c, 16)
+    g.remote_dma_fused([write(pc[pos], off, S.arr_c1)], local_sem=S.sent)
+    g.remote_dma_fused([write(pc[1 - pos], off, S.arr_c2)], local_sem=S.sent)
 
-    te, ve = g.tensor, g.vector
-    te.wait_ge(S.ld_w, 16)
-    te.wait_ge(S.ld_own, 16)
-    te.matmul(T.p_own[:, 0:B], T.ws[:], T.xs[:, c_me], True, True).then_inc(S.mm_own, 1)
-    te.wait_ge(S.arr_nb, e_nb)
-    te.matmul(T.p_nb[:, 0:B], T.ws[:], T.land[:, c_nb], True, True).then_inc(S.mm_nb, 1)
-    te.wait_ge(S.arr_far, e_far * len(far))
-    te.matmul(T.p_far[:, 0:len(far) * B], T.ws[:], T.land[:, c_far], True, True).then_inc(S.mm_far, 1)
-    te.wait_ge(S.arr_near, e_near * len(near))
-    te.matmul(T.p_near[:, 0:len(near) * B], T.ws[:], T.land[:, c_near], True, True).then_inc(S.mm_near, 1)
+    work = {"own": ([rank], 0), "ga": (pa, 2 * h), "nb": ([nb], len(on)), "gb": (pb, 2 * h),
+            "c1": ([pc[pos]], len(off)), "c2": ([pc[1 - pos]], len(off))}
+    g.tensor.wait_ge(S.ld_w, 16)
+    g.tensor.wait_ge(S.ld_own, 16)
+    for n in GROUPS:
+        ranks, count = work[n]
+        src = T.xs if n == "own" else T.land
+        acc = T["p_" + n][:, 0:len(ranks) * B]
+        if count:
+            g.tensor.wait_ge(S["arr_" + n], count)
+        g.tensor.matmul(acc, T.ws[:], src[:, _cols(ranks)], True, True).then_inc(S["mm_" + n], 1)
+        g.vector.wait_ge(S["mm_" + n], 1)
+        g.vector.tensor_copy(T.ys[:, _cols(ranks)], acc).then_inc(S["cp_" + n], 1)
 
-    ve.wait_ge(S.mm_own, 1)
-    ve.tensor_copy(T.ys[:, c_me], T.p_own[:, 0:B]).then_inc(S.cp_own, 1)
-    ve.wait_ge(S.mm_nb, 1)
-    ve.tensor_copy(T.ys[:, c_nb], T.p_nb[:, 0:B]).then_inc(S.cp_nb, 1)
-    ve.wait_ge(S.mm_far, 1)
-    ve.tensor_copy(T.ys[:, c_far], T.p_far[:, 0:len(far) * B]).then_inc(S.cp_far, 1)
-    ve.wait_ge(S.mm_near, 1)
-    ve.tensor_copy(T.ys[:, c_near], T.p_near[:, 0:len(near) * B]).then_inc(S.cp_near, 1)
+    def store(q, ranks, after, sem):
+        for n in after:
+            q.wait_ge(S["cp_" + n], 1)
+        q.dma_start(T.y[:, _cols(ranks)], T.ys[:, _cols(ranks)]).then_inc(sem, 16)
 
-    g.scalar.wait_ge(S.cp_own, 1)
-    g.scalar.wait_ge(S.cp_nb, 1)
-    g.scalar.dma_start(T.y[:, c_loc], T.ys[:, c_loc]).then_inc(S.st_loc, 16)
-    g.sync.wait_ge(S.cp_far, 1)
-    g.sync.dma_start(T.y[:, c_far], T.ys[:, c_far]).then_inc(S.st_far, 16)
-    g.sync.wait_ge(S.cp_near, 1)
-    g.sync.dma_start(T.y[:, c_near], T.ys[:, c_near]).then_inc(S.st_near, 16)
+    store(g.sync, pa, ["ga"], S.st_ga)
+    store(g.scalar, home, ["own", "nb"], S.st_loc)
+    store(g.sync, pb, ["gb"], S.st_gb)
+    store(g.scalar, [pc[pos]], ["c1"], S.st_c1)
+    store(g.sync, [pc[1 - pos]], ["c2"], S.st_c2)
 
-    g.wait_ge(S.sent, e_far * len(far) + e_near * len(near) + e_nb)
+    g.wait_ge(S.sent, 2 * h + 2 * h + len(on) + 2 * len(off))
     g.scalar.wait_ge(S.st_loc, 16)
-    g.sync.wait_ge(S.st_far, 16)
-    g.sync.wait_ge(S.st_near, 16)
+    g.scalar.wait_ge(S.st_c1, 16)
+    g.sync.wait_ge(S.st_ga, 16)
+    g.sync.wait_ge(S.st_gb, 16)
+    g.sync.wait_ge(S.st_c2, 16)

from concourse.bass import DstId, RemoteDMATransfer

N = 8
B = 128
GROUPS = ["own", "ga", "nb", "gb", "c1", "c2"]

SCRATCH = {
    "xs": ("sbuf", [128, N * B], "bfloat16"),
    "ws": ("sbuf", [128, B], "bfloat16"),
    "land": ("sbuf", [128, N * B], "bfloat16"),
    "ys": ("sbuf", [128, N * B], "bfloat16"),
}
for _n in GROUPS:
    SCRATCH["p_" + _n] = ("psum", [128, 512], "float32")
SEMAPHORES = (["ld_a", "ld_own", "ld_c", "ld_w", "sent", "st_loc"]
              + ["arr_" + n for n in GROUPS[1:]] + ["mm_" + n for n in GROUPS] + ["cp_" + n for n in GROUPS]
              + ["st_" + n for n in GROUPS if n not in ("own", "nb")])


def _bits(mask):
    return [b for b in range(16) if (mask >> b) & 1]


def _mask(engines):
    m = 0
    for b in engines:
        m |= 1 << b
    return m


def _cols(ranks):
    lo, hi = min(ranks), max(ranks)
    assert hi - lo + 1 == len(ranks)
    return slice(lo * B, (hi + 1) * B)


def _plan(rank, cores, topo):
    chips = []
    for c in cores:
        if topo.chip(c) not in chips:
            chips.append(topo.chip(c))
    members = [[r for r in range(N) if topo.chip(cores[r]) == ch] for ch in chips]
    assert len(chips) == 4 and all(len(m) == 2 for m in members)

    def hops(d):
        return max(1 if topo.same_plane(chips[i], chips[i ^ d]) or topo.mates(chips[i], chips[i ^ d]) else 2
                   for i in range(4))

    rounds = sorted([1, 2, 3], key=lambda d: (-hops(d), -d))
    i = chips.index(topo.chip(cores[rank]))
    return members[i], [members[i ^ d] for d in rounds], members[i].index(rank)


def rank_program(g, core, T, topo):
    rank = T.rank_of(core)
    if rank is None:
        return
    cores = list(T.cores)
    S = T.sem
    home, (pa, pb, pc), pos = _plan(rank, cores, topo)
    nb = home[1 - pos]
    assert all(topo.may_write(core, cores[r]) for r in range(N) if r != rank)

    off = _bits(topo.mask(core, cores[pa[0]]))
    assert all(_bits(topo.mask(core, cores[r])) == off for r in pa + pb + pc)
    on = [b for b in _bits(topo.mask(core, cores[nb])) if b not in off][:4]
    h = len(off) // 2

    def write(dst_rank, engines, sem):
        rid, pid, _ = topo.addr(cores[dst_rank])
        return RemoteDMATransfer(dst_ids=[DstId(rid=rid, pnc=pid)], dma_engine_mask=_mask(engines), remote_sem=sem,
                                 src=T.xs[:, _cols([dst_rank])], dst=T.land[:, _cols([rank])])

    for ranks, sem in ((pa, S.ld_a), (home + pb, S.ld_own), (pc, S.ld_c)):
        g.sync.dma_start(T.xs[:, _cols(ranks)], T.x[:, _cols(ranks)]).then_inc(sem, 16)
    g.sync.dma_start(T.ws[:], T.w[:]).then_inc(S.ld_w, 16)

    g.wait_ge(S.ld_a, 16)
    g.remote_dma_fused([write(pa[0], off[:h], S.arr_ga), write(pa[1], off[h:], S.arr_ga)], local_sem=S.sent)
    g.wait_ge(S.ld_own, 16)
    g.remote_dma_fused([write(pb[0], off[:h], S.arr_gb), write(pb[1], off[h:], S.arr_gb), write(nb, on, S.arr_nb)],
                       local_sem=S.sent)
    g.wait_ge(S.ld_c, 16)
    g.remote_dma_fused([write(pc[pos], off, S.arr_c1)], local_sem=S.sent)
    g.remote_dma_fused([write(pc[1 - pos], off, S.arr_c2)], local_sem=S.sent)

    work = {"own": ([rank], 0), "ga": (pa, 2 * h), "nb": ([nb], len(on)), "gb": (pb, 2 * h),
            "c1": ([pc[pos]], len(off)), "c2": ([pc[1 - pos]], len(off))}
    g.tensor.wait_ge(S.ld_w, 16)
    g.tensor.wait_ge(S.ld_own, 16)
    for n in GROUPS:
        ranks, count = work[n]
        src = T.xs if n == "own" else T.land
        acc = T["p_" + n][:, 0:len(ranks) * B]
        if count:
            g.tensor.wait_ge(S["arr_" + n], count)
        g.tensor.matmul(acc, T.ws[:], src[:, _cols(ranks)], True, True).then_inc(S["mm_" + n], 1)
        g.vector.wait_ge(S["mm_" + n], 1)
        g.vector.tensor_copy(T.ys[:, _cols(ranks)], acc).then_inc(S["cp_" + n], 1)

    def store(q, ranks, after, sem):
        for n in after:
            q.wait_ge(S["cp_" + n], 1)
        q.dma_start(T.y[:, _cols(ranks)], T.ys[:, _cols(ranks)]).then_inc(sem, 16)

    store(g.sync, pa, ["ga"], S.st_ga)
    store(g.scalar, home, ["own", "nb"], S.st_loc)
    store(g.sync, pb, ["gb"], S.st_gb)
    store(g.scalar, [pc[pos]], ["c1"], S.st_c1)
    store(g.sync, [pc[1 - pos]], ["c2"], S.st_c2)

    g.wait_ge(S.sent, 2 * h + 2 * h + len(on) + 2 * len(off))
    g.scalar.wait_ge(S.st_loc, 16)
    g.scalar.wait_ge(S.st_c1, 16)
    g.sync.wait_ge(S.st_ga, 16)
    g.sync.wait_ge(S.st_gb, 16)
    g.sync.wait_ge(S.st_c2, 16)
